import numpy as np, ml_dtypes
CORES = [29,45,93,109,157,173,221,237,285,301,349,365,413,429,477,493]
N = 16
import mx_ref
NC, KT, ROOT = 512, 1, 6
BF = ml_dtypes.bfloat16
def setup_inputs(rng):
    def f(*shape):
        return mx_ref.flush((rng.standard_normal(shape, dtype=np.float32) * np.exp2(rng.integers(-2, 3, shape[:-1] + (1,)))).astype(BF))
    return {"w": f(N, 128, KT * 512), "x": f(N, 128, KT * 4 * NC)}
def setup_inputs_blocks(rng):
    d = setup_inputs(rng)
    for k in ("w", "x"): d[k] = mx_ref.spread(d[k], rng, 4)
    return d
def setup_inputs_wide(rng):
    d = setup_inputs(rng)
    for k in ("w", "x"): d[k] = mx_ref.flush((d[k].astype(np.float32) * np.exp2(rng.integers(-8, 9, (N, 1, 1))).astype(np.float32)).astype(BF))
    return d
def setup_inputs_zeros(rng):
    d = setup_inputs(rng); v = d["x"].reshape(N, 128, -1, 4).copy()
    v[np.broadcast_to((rng.random((N, 1, v.shape[2], 1)) < 0.33), v.shape)] = 0
    d["x"] = v.reshape(d["x"].shape)
    return d
def reference(w, x):
    QW = [mx_ref.quantize(w[ROOT][:, 512 * t:512 * t + 512]) for t in range(KT)]
    y = np.zeros((N, 128, NC), np.float32)
    for r in range(N):
        for t in range(KT):
            p = mx_ref.matmul(QW[t], mx_ref.quantize(x[r][:, 4 * NC * t:4 * NC * t + 4 * NC]))
            y[r] = p if t == 0 else y[r] + p
    return {"y": y}

from concourse.bass import DstId, RemoteDMATransfer
from concourse.mybir import dt, ActivationFunctionType

SCRATCH = {
    "wb": ("sbuf", [128, 512], "bfloat16"),
    "xb": ("sbuf", [128, 2048], "bfloat16"),
    "wq": ("sbuf", [128, 128], "float8_e4m3fn_x4"),
    "ws": ("sbuf", [128, 128], "uint8"),
    "xq": ("sbuf", [128, 512], "float8_e4m3fn_x4"),
    "xs": ("sbuf", [128, 512], "uint8"),
    "ps": ("psum", [128, 1024], "float32"),
    "yb": ("sbuf", [128, 512], "float32"),
}
SEMAPHORES = ["wl", "xl", "wqd", "xqd", "sc", "cd", "sent", "mma", "mmb", "cp", "st"]


def _bits(mask):
    return bin(mask).count("1")


def _plan(T, topo):
    cores = list(T.cores)
    root = cores[T.root]

    def cabled(a, b):
        return (topo.rack(topo.host(a)) != topo.rack(topo.host(b)) and topo.may_write(a, b)
                and topo.chip(a) == topo.chip(b))

    others = [c for c in cores if c != root]
    gate = [c for c in others if cabled(root, c)][0]
    far = [c for c in others if not topo.may_write(root, c)]
    home = [c for c in others if topo.host(c) == topo.host(root)]
    near = [c for c in others if topo.same_plane(root, c) and c not in home]
    kids = {gate: [c for c in far if topo.same_plane(gate, c)]}
    for h in home:
        kids[h] = [c for c in others if cabled(h, c)]
    first = [gate] + home
    n = len(first) + 1
    left = list(near)
    for k, r in enumerate(first):
        while left[1:] and len(kids[r]) < n - (k + 1):
            kids[r].append(left.pop(0))
    kids[root] = first + left
    return {s: [(topo.mask(s, d[0]), d)] for s, d in kids.items() if d}


def rank_program(g, core, T, topo):
    plan = _plan(T, topo)
    root = T.cores[T.root]
    rank = T.rank_of(core)
    arrive = 0
    for s, groups in plan.items():
        for mask, dsts in groups:
            if core in dsts:
                arrive = _bits(mask)
    if rank is None and core not in plan and not arrive:
        return

    if core == root:
        g.sync.dma_start(T.wb[:], T.w[:]).then_inc(T.sem.wl, 16)
    if rank is not None:
        g.sync.dma_start(T.xb[:], T.x[:]).then_inc(T.sem.xl, 16)
    if core == root:
        g.vector.wait_ge(T.sem.wl, 16)
        g.vector.quantize_mx(T.wq[:], T.ws[:], T.wb[:]).then_inc(T.sem.wqd, 1)
    if rank is not None:
        g.vector.wait_ge(T.sem.xl, 16)
        g.vector.quantize_mx(T.xq[:], T.xs[:], T.xb[:]).then_inc(T.sem.xqd, 1)

    groups = plan.get(core, [])
    if groups:
        sent = 0
        for piece in ("plane", "codes"):
            if core == root:
                g.wait_ge(T.sem.wqd, 1)
            else:
                g.wait_ge(T.sem.sc if piece == "plane" else T.sem.cd, arrive)
            ap = T.ws[:] if piece == "plane" else T.wq[:].bitcast(dt.uint8)
            transfers = []
            for mask, dsts in groups:
                ids = []
                for d in dsts:
                    rid, pid = topo.addr(d, core)
                    ids.append(DstId(rid=rid, pnc=pid))
                transfers.append(RemoteDMATransfer(
                    dst_ids=ids, dma_engine_mask=mask,
                    remote_sem=T.sem.sc if piece == "plane" else T.sem.cd,
                    srcs=[ap], dsts=[ap for _ in dsts]))
                sent += _bits(mask)
            g.remote_dma_fused(transfers, local_sem=T.sem.sent)
        g.wait_ge(T.sem.sent, sent)

    if rank is None:
        return

    g.tensor.wait_ge(T.sem.xqd, 1)
    if core == root:
        g.tensor.wait_ge(T.sem.wqd, 1)
    else:
        g.tensor.wait_ge(T.sem.sc, arrive)
        g.tensor.wait_ge(T.sem.cd, arrive)
    g.tensor.matmul_mx(T.ps[:, 0:256], T.wq[:], T.ws[:], T.xq[:, 0:256], T.xs[:, 0:256], True, True).then_inc(T.sem.mma, 1)
    g.tensor.matmul_mx(T.ps[:, 512:768], T.wq[:], T.ws[:], T.xq[:, 256:512], T.xs[:, 256:512], True, True).then_inc(T.sem.mmb, 1)
    g.vector.wait_ge(T.sem.mma, 1)
    g.vector.tensor_copy(T.yb[:, 0:256], T.ps[:, 0:256]).then_inc(T.sem.cp, 1)
    g.scalar.wait_ge(T.sem.mmb, 1)
    g.scalar.activation(T.yb[:, 256:512], T.ps[:, 512:768], ActivationFunctionType.Copy).then_inc(T.sem.cp, 1)
    g.sync.wait_ge(T.sem.cp, 2)
    g.sync.dma_start(T.y[:], T.yb[:]).then_inc(T.sem.st, 16)
    g.sync.wait_ge(T.sem.st, 16)
